import numpy as np
import ml_dtypes


def mxq(x, axis, fmt="e4m3"):
    dtype, down = {"e4m3": (ml_dtypes.float8_e4m3fn, 7), "e5m2": (ml_dtypes.float8_e5m2, 14)}[fmt]
    v = np.moveaxis(np.asarray(x, np.float32).astype(ml_dtypes.bfloat16).astype(np.float64), axis, -1)
    blocks = v.reshape(v.shape[:-1] + (-1, 32))
    amax = np.abs(blocks).max(-1, keepdims=True)
    byte = np.maximum(np.where(amax > 0, np.frexp(amax)[1] - 1 + 127, 0) - down, 1)
    scale = np.exp2(byte - 127.0)
    codes = (blocks / scale).astype(np.float32).astype(dtype).astype(np.float64)
    return np.moveaxis((codes * scale).reshape(v.shape), -1, axis)


WIDE = False


def mx_kscale(k):
    if not WIDE:
        return np.ones(k)
    levels = np.array([10, -10, 5, -5, 0])
    if k % 512:
        return np.exp2(np.random.permutation(np.resize(levels, k // 32))).repeat(32)
    a = np.empty((k // 512, 16))
    for p in range(k // 512):
        a[p, :8] = np.random.permutation(np.resize(levels, 8))
        for g in range(8):
            far = levels[np.abs(levels - a[p, g]) >= 10]
            a[p, g + 8] = far[np.random.randint(len(far))]
    return np.exp2(a.ravel()).repeat(32)


def f64(x):
    return np.asarray(x).astype(np.float64)


def striped(idx):
    return np.tile(np.asarray(idx).reshape(-1, 16).T, (8, 1)).astype(np.uint16)


def unstriped(offs):
    return offs[:16].T.reshape(-1).astype(np.int64)


E2M1 = np.array([0.0, 0.5, 1.0, 1.5, 2.0, 3.0, 4.0, 6.0, -0.0, -0.5, -1.0, -1.5, -2.0, -3.0, -4.0, -6.0])


def pack_weight(w, fmt):
    k, n = w.shape
    w = f64(np.asarray(w, np.float32).astype(ml_dtypes.bfloat16)).reshape(k // 32, 32, n)
    amax = np.abs(w).max(1)
    if fmt == "e4m3":
        byte = np.frexp(amax)[1] - 1 + 127 - 7
    else:
        mant, ex = np.frexp(amax / 6.0)
        byte = np.where(mant > 0.5, ex, ex - 1) + 127
    byte = np.clip(np.where(amax > 0, byte, 1), 1, 254)
    scaled = (w * np.exp2(127.0 - byte)[:, None, :]).reshape(k, n).astype(np.float32)
    by_word = np.ascontiguousarray(scaled.reshape(k // 512, 128, 4, n).transpose(0, 1, 3, 2))
    if fmt == "e4m3":
        words = by_word.astype(ml_dtypes.float8_e4m3fn).view(np.uint8)
    else:
        c = by_word.astype(ml_dtypes.float4_e2m1fn).view(np.uint8) & 0xF
        words = (c[..., 0::2] | (c[..., 1::2] << 4)).reshape(k // 512, 128, 2 * n)
    return np.ascontiguousarray(words), np.ascontiguousarray(byte.astype(np.uint8).reshape(k // 512, 16, n))


def unpack_weight(words, scales, fmt):
    g, _, n = scales.shape
    words = np.ascontiguousarray(words).reshape(g, 128, n, -1)
    if fmt == "e4m3":
        vals = words.view(ml_dtypes.float8_e4m3fn).astype(np.float64)
    else:
        nib = np.empty((g, 128, n, 4), np.uint8)
        nib[..., 0::2] = words & 0xF
        nib[..., 1::2] = words >> 4
        vals = E2M1[nib]
    vals = vals * np.repeat(np.exp2(scales.astype(np.float64) - 127.0), 8, axis=1)[..., None]
    return vals.transpose(0, 1, 3, 2).reshape(g * 512, n)


K, T, J, N = 1024, 2048, 512, 512


def setup_inputs():
    n = np.random.standard_normal
    idx = np.random.permutation(T)[:J]
    idx2 = np.random.permutation(T)[:J]
    fk = mx_kscale(K)
    xtp = pack_weight(n((K, T)) * np.random.uniform(0.3, 1.7, (1, T)) / fk[:, None], "e4m3")
    wbp = pack_weight(n((K, N)) * 1 / np.sqrt(K) * fk[:, None], "e2m1")
    return {
        "xt_words": xtp[0],
        "xt_scales": xtp[1],
        "wa": (n((K, N)) * 1 / np.sqrt(K) * fk[:, None]).astype(np.float32),
        "wb_words": wbp[0],
        "wb_scales": wbp[1],
        "bi": (np.random.uniform(-1.0, 1.0, (1, N))).astype(np.float32),
        "offs": striped(idx),
        "offs2": striped(idx2),
    }


def reference(xt_words, xt_scales, wa, wb_words, wb_scales, bi, offs, offs2):
    idx = unstriped(offs)
    idx2 = unstriped(offs2)
    xtu = unpack_weight(xt_words, xt_scales, "e4m3")
    wbu = unpack_weight(wb_words, wb_scales, "e2m1")
    xtidxg = xtu[:, idx]
    waq = mxq(f64(wa), 0, "e4m3")
    a0 = xtidxg.T @ waq
    xtidx2g = xtu[:, idx2]
    b0 = xtidx2g.T @ wbu
    a = a0 + f64(bi)
    b = b0 + f64(bi)
    y = a - b * np.mean(a * b, axis=1, keepdims=True) / (np.mean(np.square(b), axis=1, keepdims=True) + 0.1)
    return y

@@ -1,0 +1,200 @@
+from contextlib import ExitStack
+
+import concourse.mybir as mybir
+from concourse.masks import make_identity
+
+K, T, J, N = 1024, 2048, 512, 512
+FLOPS = 2 * 2 * K * J * N
+
+F32 = mybir.dt.float32
+BF16 = mybir.dt.bfloat16
+I32 = mybir.dt.int32
+U32 = mybir.dt.uint32
+U16 = mybir.dt.uint16
+U8 = mybir.dt.uint8
+FP8X4 = mybir.dt.float8_e4m3fn_x4
+FP4X4 = mybir.dt.float4_e2m1fn_x4
+ALU = mybir.AluOpType
+ACT = mybir.ActivationFunctionType
+
+P = 128
+PACK = 4
+PASSES = K // (P * PACK)
+BLOCKS = J // P
+HALF = N // 2
+QUADRANTS = 4
+LEAD = 512
+
+
+def tile_moe_expert_less_common_part_kernel(tc, xt_words, xt_scales, wa, wb_words, wb_scales, bi, offs, offs2, out):
+    nc = tc.nc
+    with ExitStack() as ctx:
+        keep = ctx.enter_context(tc.tile_pool(name="keep", bufs=1))
+        psum = ctx.enter_context(tc.psum_pool(name="psum", bufs=1))
+
+        list_a = keep.tile([P, J // 16], U16, name="list_a")
+        list_b = keep.tile([P, J // 16], U16, name="list_b")
+        x_planes = keep.tile([P, T], U8, name="x_planes", align_bytes=64)
+        wb_planes = keep.tile([P, PASSES, N], U8, name="wb_planes", align_bytes=64)
+        xb_plane1 = keep.tile([P, J], U8, name="xb_plane1", align_bytes=64)
+        nc.gpsimd.memset(x_planes[:].bitcast(I32), 0)
+        nc.vector.memset(wb_planes[:].bitcast(I32), 0)
+        nc.vector.memset(xb_plane1[:].bitcast(I32), 0)
+
+        warm = keep.tile([P, 2], F32, name="warm")
+        nc.vector.memset(warm[:, 0:1], 0.0)
+        nc.scalar.activation(out=warm[:, 1:2], in_=warm[:, 0:1], func=ACT.Square)
+        nc.sync.dma_start(list_b[:], offs2)
+        nc.sync.dma_start(list_a[:], offs)
+        x_words = [keep.tile([P, T], U32, name=f"x_words{z}", align_bytes=64) for z in range(PASSES)]
+        x_dram = [xt_words[z].rearrange("p c r -> p (c r)").bitcast(I32) for z in range(PASSES)]
+        nc.sync.dma_start(out=x_words[0][:, :LEAD].bitcast(I32), in_=x_dram[0][:, :LEAD])
+        for q in range(QUADRANTS):
+            nc.sync.dma_start(
+                out=x_planes[32 * q : 32 * q + 8, :].bitcast(I32),
+                in_=xt_scales[:, 4 * q : 4 * q + 4, :].bitcast(I32),
+            )
+        bi_cols = keep.tile([P, N // P], F32, name="bi_cols")
+        nc.sync.dma_start(out=x_words[0][:, LEAD:].bitcast(I32), in_=x_dram[0][:, LEAD:])
+        for q in range(QUADRANTS):
+            nc.sync.dma_start(
+                out=wb_planes[32 * q : 32 * q + 4, :, :].bitcast(I32),
+                in_=wb_scales[:, 4 * q : 4 * q + 4, :].rearrange("z r c -> r z c").bitcast(I32),
+            )
+        chunks = [(z, h) for h in range(2) for z in range(PASSES)]
+        wa_raw = {}
+
+        def load_wa(z, h):
+            wa_raw[z, h] = keep.tile([P, PACK, HALF], F32, name=f"wa_raw{z}{h}", tag=f"raw{z}{h}", align_bytes=64)
+            rows = wa[z * P * PACK : (z + 1) * P * PACK, h * HALF : (h + 1) * HALF]
+            nc.sync.dma_start(out=wa_raw[z, h][:], in_=rows.rearrange("(p t) c -> p t c", t=PACK))
+
+        load_wa(*chunks[0])
+        with nc.allow_non_contiguous_dma(reason="one offset a partition"):
+            nc.sync.dma_start(out=bi_cols[:], in_=bi[0].rearrange("(m p) -> p m", p=P))
+        nc.sync.dma_start(out=x_words[1][:].bitcast(I32), in_=x_dram[1])
+        wb_codes = keep.tile([P, PASSES, 2 * N], U8, name="wb_codes", align_bytes=64)
+        nc.sync.dma_start(out=wb_codes[:].bitcast(I32), in_=wb_words.rearrange("z p c -> p z c").bitcast(I32))
+        for chunk in chunks[1:]:
+            load_wa(*chunk)
+
+        banks = [psum.tile([P, N], F32, name=f"bank{i}") for i in range(8)]
+
+        ident = keep.tile([P, P], F32, name="ident")
+        make_identity(nc, ident[:])
+        bias_ps = banks[7]
+        for t in range(PACK):
+            nc.tensor.transpose(bias_ps[:, t * P : (t + 1) * P], bi_cols[:, t : t + 1].to_broadcast([P, P]), ident[:])
+        bias = keep.tile([P, N], F32, name="bias")
+        nc.scalar.copy(out=bias[:], in_=bias_ps[:])
+
+        xb_planes = keep.tile([P, J], U8, name="xb_planes", align_bytes=64)
+        xa_planes = keep.tile([P, J], U8, name="xa_planes", align_bytes=64)
+        nc.vector.tensor_copy(xb_planes[:], x_planes[:].indirect(list_b[:]))
+        nc.scalar.dma_start(out=xb_plane1[0:112, :].bitcast(I32), in_=xb_planes[4:116, :].bitcast(I32))
+        nc.vector.tensor_copy(xa_planes[:], x_planes[:].indirect(list_a[:]))
+        xa_words = [keep.tile([P, J], U32, name=f"xa_words{z}", align_bytes=64) for z in range(PASSES)]
+        xb_words = [keep.tile([P, J], U32, name=f"xb_words{z}", align_bytes=64) for z in range(PASSES)]
+        for z in range(PASSES):
+            nc.vector.tensor_copy(xb_words[z][:], x_words[z][:].indirect(list_b[:]))
+            nc.vector.tensor_copy(xa_words[z][:], x_words[z][:].indirect(list_a[:]))
+
+        b_scale = [xb_planes, xb_plane1]
+        b_sb = []
+        for z in range(PASSES):
+            for j in range(BLOCKS):
+                slots = slice(j * P, (j + 1) * P)
+                nc.tensor.matmul_mx(
+                    out=banks[j][:],
+                    lhsT=xb_words[z][:, slots].bitcast(FP8X4),
+                    lhsT_scale=b_scale[z][:, slots],
+                    rhs=wb_codes[:, z, :].bitcast(FP4X4),
+                    rhs_scale=wb_planes[:, z, :],
+                    start=(z == 0),
+                    stop=(z == PASSES - 1),
+                )
+        groups = [(0,), (1,), (2, 3)]
+        nrec_of = {}
+        bb = {g: keep.tile([P, len(g)], F32, name=f"bb{g[0]}") for g in groups}
+
+        def add_bias(j, where):
+            b_sb.append(where)
+            nc.vector.tensor_tensor(where, banks[j][:], bias[:], ALU.add)
+
+        b_early = keep.tile([P, 2, N], F32, name="b_early")
+        add_bias(0, b_early[:, 0, :])
+        add_bias(1, b_early[:, 1, :])
+
+        wa_codes = {}
+        wa_planes = {}
+        a_turned = {}
+        den = {g: keep.tile([P, len(g)], F32, name=f"den{g[0]}") for g in groups}
+        nrec = {g: keep.tile([P, len(g)], F32, name=f"nrec{g[0]}") for g in groups}
+        for z, h in chunks:
+            wa_codes[z, h] = keep.tile([P, HALF], U32, name=f"wa_codes{z}{h}", align_bytes=64)
+            wa_planes[z, h] = keep.tile([P, HALF], U8, name=f"wa_planes{z}{h}", align_bytes=64)
+            grouped = keep.tile([P, HALF, PACK], BF16, name=f"grouped{z}{h}", tag=f"stage{z}{h}", align_bytes=64)
+            dst = grouped[:].rearrange("p (c i) t -> p c t i", i=4)
+            src = wa_raw[z, h][:].rearrange("p t (c i) -> p c t i", i=4)
+            if (z, h) == chunks[-1]:
+                nc.vector.tensor_copy(out=dst, in_=src)
+            else:
+                nc.scalar.copy(out=dst, in_=src)
+            nc.vector.quantize_mx(
+                out=wa_codes[z, h][:].bitcast(FP8X4),
+                scales=wa_planes[z, h][:],
+                in_=grouped[:].rearrange("p c t -> p (c t)"),
+            )
+            for u in range(2):
+                cols = slice(u * P, (u + 1) * P)
+                nc.tensor.matmul_mx(
+                    out=banks[BLOCKS + 2 * h + u][:],
+                    lhsT=wa_codes[z, h][:, cols].bitcast(FP8X4),
+                    lhsT_scale=wa_planes[z, h][:, cols],
+                    rhs=xa_words[z][:].bitcast(FP8X4),
+                    rhs_scale=xa_planes[4 * z : P, :],
+                    start=(z == 0),
+                    stop=(z == PASSES - 1),
+                )
+        a_banks = banks[BLOCKS:]
+        early = keep.tile([P, 2, J], F32, name="early", tag="raw01", align_bytes=64)
+        for m in range(N // P):
+            a_turned[m] = early[:, m, :] if m < 2 else keep.tile([P, J], F32, name=f"a_turned{m}")[:]
+            if m == 2:
+                nc.vector.tensor_scalar(a_turned[m], banks[BLOCKS + m][:], bi_cols[:, m : m + 1], None, ALU.add)
+            else:
+                nc.scalar.activation(out=a_turned[m], in_=banks[BLOCKS + m][:], func=ACT.Identity, bias=bi_cols[:, m : m + 1])
+        late = keep.tile([P, 2, N], F32, name="late", tag="raw11", align_bytes=64)
+        add_bias(2, late[:, 0, :])
+        add_bias(3, late[:, 1, :])
+        turns = [(j, m) for j in range(2) for m in range(2)]
+        turns += [(j, m) for j in range(BLOCKS) for m in range(N // P) if (j, m) not in turns]
+        for j, m in turns:
+            nc.tensor.transpose(a_banks[j][:, m * P : (m + 1) * P], a_turned[m][:, j * P : (j + 1) * P], ident[:])
+        spent_tags = ["stage10", "stage11", "stage00", "stage01"]
+        for group in groups:
+            for j in group:
+                squares = keep.tile([P, N], F32, name=f"squares{j}", tag=spent_tags[j], align_bytes=64)
+                at = j - group[0]
+                nc.scalar.activation(out=squares[:], in_=b_sb[j], func=ACT.Square, accum_out=bb[group][:, at : at + 1])
+                nrec_of[j] = nrec[group][:, at : at + 1]
+            nc.vector.tensor_scalar(den[group][:], bb[group][:], -1.0, -0.1 * N, ALU.mult, ALU.add)
+            nc.vector.reciprocal(nrec[group][:], den[group][:])
+
+        negc = [keep.tile([P, 1], F32, name=f"negc{j}") for j in range(BLOCKS)]
+        y = [keep.tile([P, N], F32, name=f"y{j}") for j in range(BLOCKS)]
+
+        def project(j):
+            nc.vector.scalar_tensor_tensor(
+                y[j][:], a_banks[j][:], nrec_of[j], b_sb[j], ALU.mult, ALU.mult, accum_out=negc[j][:]
+            )
+
+        def finish(j):
+            nc.vector.scalar_tensor_tensor(y[j][:], b_sb[j], negc[j][:], a_banks[j][:], ALU.mult, ALU.add)
+            nc.sync.dma_start(out=out[j * P : (j + 1) * P, :], in_=y[j][:])
+
+        for step in range(BLOCKS + 1):
+            if step < BLOCKS:
+                project(step)
+            if step >= 1:
+                finish(step - 1)

@@ -34,16 +34,18 @@ def tile_moe_expert_less_common_part_kernel(tc, xt_words, xt_scales, wa, wb_word
 
         list_a = keep.tile([P, J // 16], U16, name="list_a")
         list_b = keep.tile([P, J // 16], U16, name="list_b")
-        x_planes = keep.tile([P, T], U8, name="x_planes", align_bytes=64)
+        x_planes = keep.tile([P, T], U8, name="x_planes", tag="x_planes", align_bytes=64)
         wb_planes = keep.tile([P, PASSES, N], U8, name="wb_planes", align_bytes=64)
         xb_plane1 = keep.tile([P, J], U8, name="xb_plane1", align_bytes=64)
         nc.gpsimd.memset(x_planes[:].bitcast(I32), 0)
-        nc.vector.memset(wb_planes[:].bitcast(I32), 0)
-        nc.vector.memset(xb_plane1[:].bitcast(I32), 0)
-
         warm = keep.tile([P, 2], F32, name="warm")
         nc.vector.memset(warm[:, 0:1], 0.0)
         nc.scalar.activation(out=warm[:, 1:2], in_=warm[:, 0:1], func=ACT.Square)
+        bi_rows = keep.tile([P, P], F32, name="bi_rows")
+        nc.vector.memset(bi_rows[:], 0.0)
+        nc.vector.memset(wb_planes[:].bitcast(I32), 0)
+        nc.vector.memset(xb_plane1[:].bitcast(I32), 0)
+
         nc.sync.dma_start(list_b[:], offs2)
         nc.sync.dma_start(list_a[:], offs)
         x_words = [keep.tile([P, T], U32, name=f"x_words{z}", align_bytes=64) for z in range(PASSES)]
@@ -56,32 +58,31 @@ def tile_moe_expert_less_common_part_kernel(tc, xt_words, xt_scales, wa, wb_word
             )
         bi_cols = keep.tile([P, N // P], F32, name="bi_cols")
         nc.sync.dma_start(out=x_words[0][:, LEAD:].bitcast(I32), in_=x_dram[0][:, LEAD:])
+        chunks = [(z, h) for h in range(2) for z in range(PASSES)]
+        wa_raw = {}
+
+        def load_wa(z, h):
+            rows = wa[z * P * PACK : (z + 1) * P * PACK, h * HALF : (h + 1) * HALF]
+            nc.sync.dma_start(out=wa_raw[z, h], in_=rows.rearrange("(p t) c -> p t c", t=PACK))
+
+        wa_raw[chunks[0]] = keep.tile([P, PACK, HALF], F32, name="wa_first")[:]
+        load_wa(*chunks[0])
+        wb_codes = keep.tile([P, PASSES, 2 * N], U8, name="wb_codes", align_bytes=64)
+        nc.sync.dma_start(out=wb_codes[:].bitcast(I32), in_=wb_words.rearrange("z p c -> p z c").bitcast(I32))
+        nc.sync.dma_start(out=x_words[1][:].bitcast(I32), in_=x_dram[1])
         for q in range(QUADRANTS):
             nc.sync.dma_start(
                 out=wb_planes[32 * q : 32 * q + 4, :, :].bitcast(I32),
                 in_=wb_scales[:, 4 * q : 4 * q + 4, :].rearrange("z r c -> r z c").bitcast(I32),
             )
-        chunks = [(z, h) for h in range(2) for z in range(PASSES)]
-        wa_raw = {}
-
-        def load_wa(z, h):
-            wa_raw[z, h] = keep.tile([P, PACK, HALF], F32, name=f"wa_raw{z}{h}", tag=f"raw{z}{h}", align_bytes=64)
-            rows = wa[z * P * PACK : (z + 1) * P * PACK, h * HALF : (h + 1) * HALF]
-            nc.sync.dma_start(out=wa_raw[z, h][:], in_=rows.rearrange("(p t) c -> p t c", t=PACK))
-
-        load_wa(*chunks[0])
-        with nc.allow_non_contiguous_dma(reason="one offset a partition"):
-            nc.sync.dma_start(out=bi_cols[:], in_=bi[0].rearrange("(m p) -> p m", p=P))
-        nc.sync.dma_start(out=x_words[1][:].bitcast(I32), in_=x_dram[1])
-        wb_codes = keep.tile([P, PASSES, 2 * N], U8, name="wb_codes", align_bytes=64)
-        nc.sync.dma_start(out=wb_codes[:].bitcast(I32), in_=wb_words.rearrange("z p c -> p z c").bitcast(I32))
-        for chunk in chunks[1:]:
-            load_wa(*chunk)
 
         banks = [psum.tile([P, N], F32, name=f"bank{i}") for i in range(8)]
 
         ident = keep.tile([P, P], F32, name="ident")
         make_identity(nc, ident[:])
+        nc.gpsimd.dma_start(out=bi_rows[0 : N // P, :], in_=bi[0].rearrange("(m c) -> m c", c=P))
+        nc.tensor.transpose(banks[6][:, 0:P], bi_rows[:], ident[:])
+        nc.scalar.copy(out=bi_cols[:], in_=banks[6][:, 0 : N // P])
         bias_ps = banks[7]
         for t in range(PACK):
             nc.tensor.transpose(bias_ps[:, t * P : (t + 1) * P], bi_cols[:, t : t + 1].to_broadcast([P, P]), ident[:])
@@ -93,6 +94,10 @@ def tile_moe_expert_less_common_part_kernel(tc, xt_words, xt_scales, wa, wb_word
         nc.vector.tensor_copy(xb_planes[:], x_planes[:].indirect(list_b[:]))
         nc.scalar.dma_start(out=xb_plane1[0:112, :].bitcast(I32), in_=xb_planes[4:116, :].bitcast(I32))
         nc.vector.tensor_copy(xa_planes[:], x_planes[:].indirect(list_a[:]))
+        wa_rest = keep.tile([P, len(chunks) - 1, PACK, HALF], F32, name="wa_rest", tag="x_planes", align_bytes=64)
+        for i, chunk in enumerate(chunks[1:]):
+            wa_raw[chunk] = wa_rest[:, i]
+            load_wa(*chunk)
         xa_words = [keep.tile([P, J], U32, name=f"xa_words{z}", align_bytes=64) for z in range(PASSES)]
         xb_words = [keep.tile([P, J], U32, name=f"xb_words{z}", align_bytes=64) for z in range(PASSES)]
         for z in range(PASSES):
@@ -135,7 +140,7 @@ def tile_moe_expert_less_common_part_kernel(tc, xt_words, xt_scales, wa, wb_word
             wa_planes[z, h] = keep.tile([P, HALF], U8, name=f"wa_planes{z}{h}", align_bytes=64)
             grouped = keep.tile([P, HALF, PACK], BF16, name=f"grouped{z}{h}", tag=f"stage{z}{h}", align_bytes=64)
             dst = grouped[:].rearrange("p (c i) t -> p c t i", i=4)
-            src = wa_raw[z, h][:].rearrange("p t (c i) -> p c t i", i=4)
+            src = wa_raw[z, h].rearrange("p t (c i) -> p c t i", i=4)
             if (z, h) == chunks[-1]:
                 nc.vector.tensor_copy(out=dst, in_=src)
             else:
@@ -157,14 +162,14 @@ def tile_moe_expert_less_common_part_kernel(tc, xt_words, xt_scales, wa, wb_word
                     stop=(z == PASSES - 1),
                 )
         a_banks = banks[BLOCKS:]
-        early = keep.tile([P, 2, J], F32, name="early", tag="raw01", align_bytes=64)
+        early = wa_raw[chunks[2]].rearrange("p (m t) c -> p m (t c)", m=2)
         for m in range(N // P):
             a_turned[m] = early[:, m, :] if m < 2 else keep.tile([P, J], F32, name=f"a_turned{m}")[:]
             if m == 2:
                 nc.vector.tensor_scalar(a_turned[m], banks[BLOCKS + m][:], bi_cols[:, m : m + 1], None, ALU.add)
             else:
                 nc.scalar.activation(out=a_turned[m], in_=banks[BLOCKS + m][:], func=ACT.Identity, bias=bi_cols[:, m : m + 1])
-        late = keep.tile([P, 2, N], F32, name="late", tag="raw11", align_bytes=64)
+        late = wa_raw[chunks[3]].rearrange("p (m t) c -> p m (t c)", m=2)
         add_bias(2, late[:, 0, :])
         add_bias(3, late[:, 1, :])
         turns = [(j, m) for j in range(2) for m in range(2)]
@@ -190,8 +195,13 @@ def tile_moe_expert_less_common_part_kernel(tc, xt_words, xt_scales, wa, wb_word
             )
 
         def finish(j):
-            nc.vector.scalar_tensor_tensor(y[j][:], b_sb[j], negc[j][:], a_banks[j][:], ALU.mult, ALU.add)
-            nc.sync.dma_start(out=out[j * P : (j + 1) * P, :], in_=y[j][:])
+            pieces = 2 if j == BLOCKS - 1 else 1
+            for i in range(pieces):
+                cols = slice(i * N // pieces, (i + 1) * N // pieces)
+                nc.vector.scalar_tensor_tensor(
+                    y[j][:, cols], b_sb[j][:, cols], negc[j][:], a_banks[j][:, cols], ALU.mult, ALU.add
+                )
+                nc.sync.dma_start(out=out[j * P : (j + 1) * P, cols], in_=y[j][:, cols])
 
         for step in range(BLOCKS + 1):
             if step < BLOCKS:

@@ -21,9 +21,16 @@ P = 128
 PACK = 4
 PASSES = K // (P * PACK)
 BLOCKS = J // P
+GROUPS = N // P
 HALF = N // 2
 QUADRANTS = 4
+QUADRANT = P // QUADRANTS
+ROWS = 4
+LINE = 4
 LEAD = 512
+SHIFTED = 112
+VECTOR_GROUP = 2
+PAD = 8
 
 
 def tile_moe_expert_less_common_part_kernel(tc, xt_words, xt_scales, wa, wb_words, wb_scales, bi, offs, offs2, out):
@@ -36,15 +43,14 @@ def tile_moe_expert_less_common_part_kernel(tc, xt_words, xt_scales, wa, wb_word
         list_b = keep.tile([P, J // 16], U16, name="list_b")
         x_planes = keep.tile([P, T], U8, name="x_planes", tag="x_planes", align_bytes=64)
         wb_planes = keep.tile([P, PASSES, N], U8, name="wb_planes", align_bytes=64)
-        xb_plane1 = keep.tile([P, J], U8, name="xb_plane1", align_bytes=64)
+        xb_shifted = keep.tile([P, J], U8, name="xb_shifted", align_bytes=64)
         nc.gpsimd.memset(x_planes[:].bitcast(I32), 0)
-        warm = keep.tile([P, 2], F32, name="warm")
-        nc.vector.memset(warm[:, 0:1], 0.0)
-        nc.scalar.activation(out=warm[:, 1:2], in_=warm[:, 0:1], func=ACT.Square)
         bi_rows = keep.tile([P, P], F32, name="bi_rows")
         nc.vector.memset(bi_rows[:], 0.0)
+        minus_tenth = keep.tile([P, 1], F32, name="minus_tenth")
+        nc.scalar.activation(out=minus_tenth[:], in_=bi_rows[:, 0:1], func=ACT.Copy, bias=-0.1 * N)
         nc.vector.memset(wb_planes[:].bitcast(I32), 0)
-        nc.vector.memset(xb_plane1[:].bitcast(I32), 0)
+        nc.vector.memset(xb_shifted[:].bitcast(I32), 0)
 
         nc.sync.dma_start(list_b[:], offs2)
         nc.sync.dma_start(list_a[:], offs)
@@ -53,12 +59,27 @@ def tile_moe_expert_less_common_part_kernel(tc, xt_words, xt_scales, wa, wb_word
         nc.sync.dma_start(out=x_words[0][:, :LEAD].bitcast(I32), in_=x_dram[0][:, :LEAD])
         for q in range(QUADRANTS):
             nc.sync.dma_start(
-                out=x_planes[32 * q : 32 * q + 8, :].bitcast(I32),
-                in_=xt_scales[:, 4 * q : 4 * q + 4, :].bitcast(I32),
+                out=x_planes[QUADRANT * q : QUADRANT * q + PASSES * ROWS, :].bitcast(I32),
+                in_=xt_scales[:, ROWS * q : ROWS * (q + 1), :].bitcast(I32),
             )
-        bi_cols = keep.tile([P, N // P], F32, name="bi_cols")
         nc.sync.dma_start(out=x_words[0][:, LEAD:].bitcast(I32), in_=x_dram[0][:, LEAD:])
+
+        def load_wb_scales(q):
+            nc.sync.dma_start(
+                out=wb_planes[QUADRANT * q : QUADRANT * q + ROWS, :, :].bitcast(I32),
+                in_=wb_scales[:, ROWS * q : ROWS * (q + 1), :].rearrange("z r c -> r z c").bitcast(I32),
+            )
+
+        for q in range(QUADRANTS // 2):
+            load_wb_scales(q)
+        nc.sync.dma_start(out=x_words[1][:].bitcast(I32), in_=x_dram[1])
+        for q in range(QUADRANTS // 2, QUADRANTS):
+            load_wb_scales(q)
+        wb_codes = keep.tile([P, PASSES, 2 * N], U8, name="wb_codes", align_bytes=64)
+        nc.sync.dma_start(out=wb_codes[:].bitcast(I32), in_=wb_words.rearrange("z p c -> p z c").bitcast(I32))
+
         chunks = [(z, h) for h in range(2) for z in range(PASSES)]
+        last_chunk = chunks[-1]
         wa_raw = {}
 
         def load_wa(z, h):
@@ -67,144 +88,159 @@ def tile_moe_expert_less_common_part_kernel(tc, xt_words, xt_scales, wa, wb_word
 
         wa_raw[chunks[0]] = keep.tile([P, PACK, HALF], F32, name="wa_first")[:]
         load_wa(*chunks[0])
-        wb_codes = keep.tile([P, PASSES, 2 * N], U8, name="wb_codes", align_bytes=64)
-        nc.sync.dma_start(out=wb_codes[:].bitcast(I32), in_=wb_words.rearrange("z p c -> p z c").bitcast(I32))
-        nc.sync.dma_start(out=x_words[1][:].bitcast(I32), in_=x_dram[1])
-        for q in range(QUADRANTS):
-            nc.sync.dma_start(
-                out=wb_planes[32 * q : 32 * q + 4, :, :].bitcast(I32),
-                in_=wb_scales[:, 4 * q : 4 * q + 4, :].rearrange("z r c -> r z c").bitcast(I32),
-            )
 
-        banks = [psum.tile([P, N], F32, name=f"bank{i}") for i in range(8)]
+        banks = [psum.tile([P, N], F32, name=f"bank{i}") for i in range(BLOCKS + GROUPS)]
+        b_banks, a_banks = banks[:BLOCKS], banks[BLOCKS:]
 
         ident = keep.tile([P, P], F32, name="ident")
         make_identity(nc, ident[:])
-        nc.gpsimd.dma_start(out=bi_rows[0 : N // P, :], in_=bi[0].rearrange("(m c) -> m c", c=P))
-        nc.tensor.transpose(banks[6][:, 0:P], bi_rows[:], ident[:])
-        nc.scalar.copy(out=bi_cols[:], in_=banks[6][:, 0 : N // P])
-        bias_ps = banks[7]
-        for t in range(PACK):
-            nc.tensor.transpose(bias_ps[:, t * P : (t + 1) * P], bi_cols[:, t : t + 1].to_broadcast([P, P]), ident[:])
+        nc.gpsimd.dma_start(out=bi_rows[0:GROUPS, :], in_=bi[0].rearrange("(m c) -> m c", c=P))
+        nc.tensor.transpose(a_banks[2][:, 0:P], bi_rows[:], ident[:])
+        bi_cols = keep.tile([P, GROUPS], F32, name="bi_cols")
+        nc.scalar.copy(out=bi_cols[:], in_=a_banks[2][:, 0:GROUPS])
+        for m in range(GROUPS):
+            nc.tensor.transpose(a_banks[3][:, m * P : (m + 1) * P], bi_cols[:, m : m + 1].to_broadcast([P, P]), ident[:])
         bias = keep.tile([P, N], F32, name="bias")
-        nc.scalar.copy(out=bias[:], in_=bias_ps[:])
+        nc.scalar.copy(out=bias[:], in_=a_banks[3][:])
 
         xb_planes = keep.tile([P, J], U8, name="xb_planes", align_bytes=64)
         xa_planes = keep.tile([P, J], U8, name="xa_planes", align_bytes=64)
         nc.vector.tensor_copy(xb_planes[:], x_planes[:].indirect(list_b[:]))
-        nc.scalar.dma_start(out=xb_plane1[0:112, :].bitcast(I32), in_=xb_planes[4:116, :].bitcast(I32))
+        nc.scalar.dma_start(
+            out=xb_shifted[0:SHIFTED, :].bitcast(I32), in_=xb_planes[ROWS : ROWS + SHIFTED, :].bitcast(I32)
+        )
         nc.vector.tensor_copy(xa_planes[:], x_planes[:].indirect(list_a[:]))
+
         wa_rest = keep.tile([P, len(chunks) - 1, PACK, HALF], F32, name="wa_rest", tag="x_planes", align_bytes=64)
         for i, chunk in enumerate(chunks[1:]):
             wa_raw[chunk] = wa_rest[:, i]
             load_wa(*chunk)
+
         xa_words = [keep.tile([P, J], U32, name=f"xa_words{z}", align_bytes=64) for z in range(PASSES)]
         xb_words = [keep.tile([P, J], U32, name=f"xb_words{z}", align_bytes=64) for z in range(PASSES)]
         for z in range(PASSES):
             nc.vector.tensor_copy(xb_words[z][:], x_words[z][:].indirect(list_b[:]))
             nc.vector.tensor_copy(xa_words[z][:], x_words[z][:].indirect(list_a[:]))
 
-        b_scale = [xb_planes, xb_plane1]
-        b_sb = []
-        for z in range(PASSES):
-            for j in range(BLOCKS):
+        xb_scales = [xb_planes, xb_shifted]
+        for j in range(BLOCKS):
+            for z in range(PASSES):
                 slots = slice(j * P, (j + 1) * P)
                 nc.tensor.matmul_mx(
-                    out=banks[j][:],
+                    out=b_banks[j][:],
                     lhsT=xb_words[z][:, slots].bitcast(FP8X4),
-                    lhsT_scale=b_scale[z][:, slots],
+                    lhsT_scale=xb_scales[z][:, slots],
                     rhs=wb_codes[:, z, :].bitcast(FP4X4),
                     rhs_scale=wb_planes[:, z, :],
                     start=(z == 0),
                     stop=(z == PASSES - 1),
                 )
-        groups = [(0,), (1,), (2, 3)]
-        nrec_of = {}
-        bb = {g: keep.tile([P, len(g)], F32, name=f"bb{g[0]}") for g in groups}
 
-        def add_bias(j, where):
-            b_sb.append(where)
-            nc.vector.tensor_tensor(where, banks[j][:], bias[:], ALU.add)
+        early_pair, late_pair = (0, 1), (2, 3)
+        b = {}
 
-        b_early = keep.tile([P, 2, N], F32, name="b_early")
-        add_bias(0, b_early[:, 0, :])
-        add_bias(1, b_early[:, 1, :])
+        def add_bias(j, home):
+            b[j] = home
+            nc.vector.tensor_tensor(home, b_banks[j][:], bias[:], ALU.add)
 
-        wa_codes = {}
-        wa_planes = {}
-        a_turned = {}
-        den = {g: keep.tile([P, len(g)], F32, name=f"den{g[0]}") for g in groups}
-        nrec = {g: keep.tile([P, len(g)], F32, name=f"nrec{g[0]}") for g in groups}
+        b_early = keep.tile([P, len(early_pair), N], F32, name="b_early")
+        for j in early_pair:
+            add_bias(j, b_early[:, j, :])
+
         for z, h in chunks:
-            wa_codes[z, h] = keep.tile([P, HALF], U32, name=f"wa_codes{z}{h}", align_bytes=64)
-            wa_planes[z, h] = keep.tile([P, HALF], U8, name=f"wa_planes{z}{h}", align_bytes=64)
+            wa_codes = keep.tile([P, HALF], U32, name=f"wa_codes{z}{h}", align_bytes=64)
+            wa_plane = keep.tile([P, HALF], U8, name=f"wa_plane{z}{h}", align_bytes=64)
             grouped = keep.tile([P, HALF, PACK], BF16, name=f"grouped{z}{h}", tag=f"stage{z}{h}", align_bytes=64)
-            dst = grouped[:].rearrange("p (c i) t -> p c t i", i=4)
-            src = wa_raw[z, h].rearrange("p t (c i) -> p c t i", i=4)
-            if (z, h) == chunks[-1]:
-                nc.vector.tensor_copy(out=dst, in_=src)
+            rounded = grouped[:].rearrange("p (c i) t -> p c t i", i=LINE)
+            raw = wa_raw[z, h].rearrange("p t (c i) -> p c t i", i=LINE)
+            if (z, h) == last_chunk:
+                nc.vector.tensor_copy(out=rounded, in_=raw)
             else:
-                nc.scalar.copy(out=dst, in_=src)
+                nc.scalar.copy(out=rounded, in_=raw)
             nc.vector.quantize_mx(
-                out=wa_codes[z, h][:].bitcast(FP8X4),
-                scales=wa_planes[z, h][:],
+                out=wa_codes[:].bitcast(FP8X4),
+                scales=wa_plane[:],
                 in_=grouped[:].rearrange("p c t -> p (c t)"),
             )
-            for u in range(2):
-                cols = slice(u * P, (u + 1) * P)
+            for u in range(HALF // P):
+                features = slice(u * P, (u + 1) * P)
                 nc.tensor.matmul_mx(
-                    out=banks[BLOCKS + 2 * h + u][:],
-                    lhsT=wa_codes[z, h][:, cols].bitcast(FP8X4),
-                    lhsT_scale=wa_planes[z, h][:, cols],
+                    out=a_banks[h * (HALF // P) + u][:],
+                    lhsT=wa_codes[:, features].bitcast(FP8X4),
+                    lhsT_scale=wa_plane[:, features],
                     rhs=xa_words[z][:].bitcast(FP8X4),
-                    rhs_scale=xa_planes[4 * z : P, :],
+                    rhs_scale=xa_planes[ROWS * z : P, :],
                     start=(z == 0),
                     stop=(z == PASSES - 1),
                 )
-        a_banks = banks[BLOCKS:]
-        early = wa_raw[chunks[2]].rearrange("p (m t) c -> p m (t c)", m=2)
-        for m in range(N // P):
-            a_turned[m] = early[:, m, :] if m < 2 else keep.tile([P, J], F32, name=f"a_turned{m}")[:]
-            if m == 2:
-                nc.vector.tensor_scalar(a_turned[m], banks[BLOCKS + m][:], bi_cols[:, m : m + 1], None, ALU.add)
+
+        first_half = wa_raw[last_chunk].rearrange("p (m t) c -> p m (t c)", m=HALF // P)
+        a_turned = {}
+        for m in range(GROUPS):
+            a_turned[m] = first_half[:, m, :] if m < HALF // P else keep.tile([P, J], F32, name=f"a_turned{m}")[:]
+            if m == VECTOR_GROUP:
+                nc.vector.tensor_scalar(a_turned[m], a_banks[m][:], bi_cols[:, m : m + 1], None, ALU.add)
             else:
-                nc.scalar.activation(out=a_turned[m], in_=banks[BLOCKS + m][:], func=ACT.Identity, bias=bi_cols[:, m : m + 1])
-        late = wa_raw[chunks[3]].rearrange("p (m t) c -> p m (t c)", m=2)
-        add_bias(2, late[:, 0, :])
-        add_bias(3, late[:, 1, :])
-        turns = [(j, m) for j in range(2) for m in range(2)]
-        turns += [(j, m) for j in range(BLOCKS) for m in range(N // P) if (j, m) not in turns]
+                nc.scalar.activation(out=a_turned[m], in_=a_banks[m][:], func=ACT.Identity, bias=bi_cols[:, m : m + 1])
+
+        late = keep.tile([P, len(late_pair) * N + PAD], F32, name="late", tag="stage11", align_bytes=64)
+        for i, j in enumerate(late_pair):
+            add_bias(j, late[:, i * N : (i + 1) * N])
+        r_of_pair = {
+            early_pair: late[:, len(late_pair) * N : len(late_pair) * N + len(early_pair)],
+            late_pair: keep.tile([P, len(late_pair)], F32, name="r_late")[:],
+        }
+
+        turns = [(j, m) for j in early_pair for m in range(HALF // P)]
+        turns += [(j, m) for j in range(BLOCKS) for m in range(GROUPS) if (j, m) not in turns]
         for j, m in turns:
             nc.tensor.transpose(a_banks[j][:, m * P : (m + 1) * P], a_turned[m][:, j * P : (j + 1) * P], ident[:])
-        spent_tags = ["stage10", "stage11", "stage00", "stage01"]
-        for group in groups:
-            for j in group:
-                squares = keep.tile([P, N], F32, name=f"squares{j}", tag=spent_tags[j], align_bytes=64)
-                at = j - group[0]
-                nc.scalar.activation(out=squares[:], in_=b_sb[j], func=ACT.Square, accum_out=bb[group][:, at : at + 1])
-                nrec_of[j] = nrec[group][:, at : at + 1]
-            nc.vector.tensor_scalar(den[group][:], bb[group][:], -1.0, -0.1 * N, ALU.mult, ALU.add)
-            nc.vector.reciprocal(nrec[group][:], den[group][:])
 
-        negc = [keep.tile([P, 1], F32, name=f"negc{j}") for j in range(BLOCKS)]
+        spent_stages = ["stage10", "stage10", "stage01", "stage00"]
+        sums = [keep.tile([P, 1], F32, name=f"sum{j}")[:] for j in early_pair] + [bi_cols[:, 3:4], bi_cols[:, 2:3]]
+        denominators = {pair: keep.tile([P, len(pair)], F32, name=f"den{pair[0]}") for pair in (early_pair, late_pair)}
+        r = {}
+        for pair in (early_pair, late_pair):
+            for i, j in enumerate(pair):
+                squares = keep.tile([P, N], F32, name=f"squares{j}", tag=spent_stages[j], align_bytes=64)
+                nc.scalar.activation(out=squares[:], in_=b[j], func=ACT.Square, accum_out=sums[j])
+                nc.gpsimd.tensor_scalar(
+                    denominators[pair][:, i : i + 1], sums[j], -1.0, minus_tenth[:], ALU.mult, ALU.add
+                )
+                r[j] = r_of_pair[pair][:, i : i + 1]
+
+        factor = [keep.tile([P, 1], F32, name=f"factor{j}") for j in range(BLOCKS)]
         y = [keep.tile([P, N], F32, name=f"y{j}") for j in range(BLOCKS)]
 
-        def project(j):
-            nc.vector.scalar_tensor_tensor(
-                y[j][:], a_banks[j][:], nrec_of[j], b_sb[j], ALU.mult, ALU.mult, accum_out=negc[j][:]
-            )
+        def invert(pair):
+            nc.vector.reciprocal(r_of_pair[pair], denominators[pair][:])
 
-        def finish(j):
-            pieces = 2 if j == BLOCKS - 1 else 1
+        def project(j):
+            nc.vector.scalar_tensor_tensor(y[j][:], a_banks[j][:], r[j], b[j], ALU.mult, ALU.mult, accum_out=factor[j][:])
+
+        def finish(j, pieces):
             for i in range(pieces):
                 cols = slice(i * N // pieces, (i + 1) * N // pieces)
                 nc.vector.scalar_tensor_tensor(
-                    y[j][:, cols], b_sb[j][:, cols], negc[j][:], a_banks[j][:, cols], ALU.mult, ALU.add
+                    y[j][:, cols], b[j][:, cols], factor[j][:], a_banks[j][:, cols], ALU.mult, ALU.add
                 )
                 nc.sync.dma_start(out=out[j * P : (j + 1) * P, cols], in_=y[j][:, cols])
 
-        for step in range(BLOCKS + 1):
-            if step < BLOCKS:
-                project(step)
-            if step >= 1:
-                finish(step - 1)
+        def finish_aside(j):
+            a_copy = keep.tile([P, N], F32, name="a_copy")
+            part = keep.tile([P, N], F32, name="part")
+            nc.scalar.copy(out=a_copy[:], in_=a_banks[j][:])
+            nc.gpsimd.tensor_scalar(part[:], b[j], factor[j][:], 0.0, ALU.mult, ALU.add)
+            nc.gpsimd.tensor_tensor(y[j][:], part[:], a_copy[:], ALU.add)
+            nc.sync.dma_start(out=out[j * P : (j + 1) * P, :], in_=y[j][:])
+
+        invert(early_pair)
+        project(0)
+        finish_aside(0)
+        project(1)
+        invert(late_pair)
+        finish(1, pieces=1)
+        project(2)
+        project(3)
+        finish(2, pieces=1)
+        finish(3, pieces=2)

from contextlib import ExitStack

import concourse.mybir as mybir
from concourse.masks import make_identity

K, T, J, N = 1024, 2048, 512, 512
FLOPS = 2 * 2 * K * J * N

F32 = mybir.dt.float32
BF16 = mybir.dt.bfloat16
I32 = mybir.dt.int32
U32 = mybir.dt.uint32
U16 = mybir.dt.uint16
U8 = mybir.dt.uint8
FP8X4 = mybir.dt.float8_e4m3fn_x4
FP4X4 = mybir.dt.float4_e2m1fn_x4
ALU = mybir.AluOpType
ACT = mybir.ActivationFunctionType

P = 128
PACK = 4
PASSES = K // (P * PACK)
BLOCKS = J // P
GROUPS = N // P
HALF = N // 2
QUADRANTS = 4
QUADRANT = P // QUADRANTS
ROWS = 4
LINE = 4
LEAD = 512
SHIFTED = 112
VECTOR_GROUP = 2
PAD = 8


def tile_moe_expert_less_common_part_kernel(tc, xt_words, xt_scales, wa, wb_words, wb_scales, bi, offs, offs2, out):
    nc = tc.nc
    with ExitStack() as ctx:
        keep = ctx.enter_context(tc.tile_pool(name="keep", bufs=1))
        psum = ctx.enter_context(tc.psum_pool(name="psum", bufs=1))

        list_a = keep.tile([P, J // 16], U16, name="list_a")
        list_b = keep.tile([P, J // 16], U16, name="list_b")
        x_planes = keep.tile([P, T], U8, name="x_planes", tag="x_planes", align_bytes=64)
        wb_planes = keep.tile([P, PASSES, N], U8, name="wb_planes", align_bytes=64)
        xb_shifted = keep.tile([P, J], U8, name="xb_shifted", align_bytes=64)
        nc.gpsimd.memset(x_planes[:].bitcast(I32), 0)
        bi_rows = keep.tile([P, P], F32, name="bi_rows")
        nc.vector.memset(bi_rows[:], 0.0)
        minus_tenth = keep.tile([P, 1], F32, name="minus_tenth")
        nc.scalar.activation(out=minus_tenth[:], in_=bi_rows[:, 0:1], func=ACT.Copy, bias=-0.1 * N)
        nc.vector.memset(wb_planes[:].bitcast(I32), 0)
        nc.vector.memset(xb_shifted[:].bitcast(I32), 0)

        nc.sync.dma_start(list_b[:], offs2)
        nc.sync.dma_start(list_a[:], offs)
        x_words = [keep.tile([P, T], U32, name=f"x_words{z}", align_bytes=64) for z in range(PASSES)]
        x_dram = [xt_words[z].rearrange("p c r -> p (c r)").bitcast(I32) for z in range(PASSES)]
        nc.sync.dma_start(out=x_words[0][:, :LEAD].bitcast(I32), in_=x_dram[0][:, :LEAD])
        for q in range(QUADRANTS):
            nc.sync.dma_start(
                out=x_planes[QUADRANT * q : QUADRANT * q + PASSES * ROWS, :].bitcast(I32),
                in_=xt_scales[:, ROWS * q : ROWS * (q + 1), :].bitcast(I32),
            )
        nc.sync.dma_start(out=x_words[0][:, LEAD:].bitcast(I32), in_=x_dram[0][:, LEAD:])

        def load_wb_scales(q):
            nc.sync.dma_start(
                out=wb_planes[QUADRANT * q : QUADRANT * q + ROWS, :, :].bitcast(I32),
                in_=wb_scales[:, ROWS * q : ROWS * (q + 1), :].rearrange("z r c -> r z c").bitcast(I32),
            )

        for q in range(QUADRANTS // 2):
            load_wb_scales(q)
        nc.sync.dma_start(out=x_words[1][:].bitcast(I32), in_=x_dram[1])
        for q in range(QUADRANTS // 2, QUADRANTS):
            load_wb_scales(q)
        wb_codes = keep.tile([P, PASSES, 2 * N], U8, name="wb_codes", align_bytes=64)
        nc.sync.dma_start(out=wb_codes[:].bitcast(I32), in_=wb_words.rearrange("z p c -> p z c").bitcast(I32))

        chunks = [(z, h) for h in range(2) for z in range(PASSES)]
        last_chunk = chunks[-1]
        wa_raw = {}

        def load_wa(z, h):
            rows = wa[z * P * PACK : (z + 1) * P * PACK, h * HALF : (h + 1) * HALF]
            nc.sync.dma_start(out=wa_raw[z, h], in_=rows.rearrange("(p t) c -> p t c", t=PACK))

        wa_raw[chunks[0]] = keep.tile([P, PACK, HALF], F32, name="wa_first")[:]
        load_wa(*chunks[0])

        banks = [psum.tile([P, N], F32, name=f"bank{i}") for i in range(BLOCKS + GROUPS)]
        b_banks, a_banks = banks[:BLOCKS], banks[BLOCKS:]

        ident = keep.tile([P, P], F32, name="ident")
        make_identity(nc, ident[:])
        nc.gpsimd.dma_start(out=bi_rows[0:GROUPS, :], in_=bi[0].rearrange("(m c) -> m c", c=P))
        nc.tensor.transpose(a_banks[2][:, 0:P], bi_rows[:], ident[:])
        bi_cols = keep.tile([P, GROUPS], F32, name="bi_cols")
        nc.scalar.copy(out=bi_cols[:], in_=a_banks[2][:, 0:GROUPS])
        for m in range(GROUPS):
            nc.tensor.transpose(a_banks[3][:, m * P : (m + 1) * P], bi_cols[:, m : m + 1].to_broadcast([P, P]), ident[:])
        bias = keep.tile([P, N], F32, name="bias")
        nc.scalar.copy(out=bias[:], in_=a_banks[3][:])

        xb_planes = keep.tile([P, J], U8, name="xb_planes", align_bytes=64)
        xa_planes = keep.tile([P, J], U8, name="xa_planes", align_bytes=64)
        nc.vector.tensor_copy(xb_planes[:], x_planes[:].indirect(list_b[:]))
        nc.scalar.dma_start(
            out=xb_shifted[0:SHIFTED, :].bitcast(I32), in_=xb_planes[ROWS : ROWS + SHIFTED, :].bitcast(I32)
        )
        nc.vector.tensor_copy(xa_planes[:], x_planes[:].indirect(list_a[:]))

        wa_rest = keep.tile([P, len(chunks) - 1, PACK, HALF], F32, name="wa_rest", tag="x_planes", align_bytes=64)
        for i, chunk in enumerate(chunks[1:]):
            wa_raw[chunk] = wa_rest[:, i]
            load_wa(*chunk)

        xa_words = [keep.tile([P, J], U32, name=f"xa_words{z}", align_bytes=64) for z in range(PASSES)]
        xb_words = [keep.tile([P, J], U32, name=f"xb_words{z}", align_bytes=64) for z in range(PASSES)]
        for z in range(PASSES):
            nc.vector.tensor_copy(xb_words[z][:], x_words[z][:].indirect(list_b[:]))
            nc.vector.tensor_copy(xa_words[z][:], x_words[z][:].indirect(list_a[:]))

        xb_scales = [xb_planes, xb_shifted]
        for j in range(BLOCKS):
            for z in range(PASSES):
                slots = slice(j * P, (j + 1) * P)
                nc.tensor.matmul_mx(
                    out=b_banks[j][:],
                    lhsT=xb_words[z][:, slots].bitcast(FP8X4),
                    lhsT_scale=xb_scales[z][:, slots],
                    rhs=wb_codes[:, z, :].bitcast(FP4X4),
                    rhs_scale=wb_planes[:, z, :],
                    start=(z == 0),
                    stop=(z == PASSES - 1),
                )

        early_pair, late_pair = (0, 1), (2, 3)
        b = {}

        def add_bias(j, home):
            b[j] = home
            nc.vector.tensor_tensor(home, b_banks[j][:], bias[:], ALU.add)

        b_early = keep.tile([P, len(early_pair), N], F32, name="b_early")
        for j in early_pair:
            add_bias(j, b_early[:, j, :])

        for z, h in chunks:
            wa_codes = keep.tile([P, HALF], U32, name=f"wa_codes{z}{h}", align_bytes=64)
            wa_plane = keep.tile([P, HALF], U8, name=f"wa_plane{z}{h}", align_bytes=64)
            grouped = keep.tile([P, HALF, PACK], BF16, name=f"grouped{z}{h}", tag=f"stage{z}{h}", align_bytes=64)
            rounded = grouped[:].rearrange("p (c i) t -> p c t i", i=LINE)
            raw = wa_raw[z, h].rearrange("p t (c i) -> p c t i", i=LINE)
            if (z, h) == last_chunk:
                nc.vector.tensor_copy(out=rounded, in_=raw)
            else:
                nc.scalar.copy(out=rounded, in_=raw)
            nc.vector.quantize_mx(
                out=wa_codes[:].bitcast(FP8X4),
                scales=wa_plane[:],
                in_=grouped[:].rearrange("p c t -> p (c t)"),
            )
            for u in range(HALF // P):
                features = slice(u * P, (u + 1) * P)
                nc.tensor.matmul_mx(
                    out=a_banks[h * (HALF // P) + u][:],
                    lhsT=wa_codes[:, features].bitcast(FP8X4),
                    lhsT_scale=wa_plane[:, features],
                    rhs=xa_words[z][:].bitcast(FP8X4),
                    rhs_scale=xa_planes[ROWS * z : P, :],
                    start=(z == 0),
                    stop=(z == PASSES - 1),
                )

        first_half = wa_raw[last_chunk].rearrange("p (m t) c -> p m (t c)", m=HALF // P)
        a_turned = {}
        for m in range(GROUPS):
            a_turned[m] = first_half[:, m, :] if m < HALF // P else keep.tile([P, J], F32, name=f"a_turned{m}")[:]
            if m == VECTOR_GROUP:
                nc.vector.tensor_scalar(a_turned[m], a_banks[m][:], bi_cols[:, m : m + 1], None, ALU.add)
            else:
                nc.scalar.activation(out=a_turned[m], in_=a_banks[m][:], func=ACT.Identity, bias=bi_cols[:, m : m + 1])

        late = keep.tile([P, len(late_pair) * N + PAD], F32, name="late", tag="stage11", align_bytes=64)
        for i, j in enumerate(late_pair):
            add_bias(j, late[:, i * N : (i + 1) * N])
        r_of_pair = {
            early_pair: late[:, len(late_pair) * N : len(late_pair) * N + len(early_pair)],
            late_pair: keep.tile([P, len(late_pair)], F32, name="r_late")[:],
        }

        turns = [(j, m) for j in early_pair for m in range(HALF // P)]
        turns += [(j, m) for j in range(BLOCKS) for m in range(GROUPS) if (j, m) not in turns]
        for j, m in turns:
            nc.tensor.transpose(a_banks[j][:, m * P : (m + 1) * P], a_turned[m][:, j * P : (j + 1) * P], ident[:])

        spent_stages = ["stage10", "stage10", "stage01", "stage00"]
        sums = [keep.tile([P, 1], F32, name=f"sum{j}")[:] for j in early_pair] + [bi_cols[:, 3:4], bi_cols[:, 2:3]]
        denominators = {pair: keep.tile([P, len(pair)], F32, name=f"den{pair[0]}") for pair in (early_pair, late_pair)}
        r = {}
        for pair in (early_pair, late_pair):
            for i, j in enumerate(pair):
                squares = keep.tile([P, N], F32, name=f"squares{j}", tag=spent_stages[j], align_bytes=64)
                nc.scalar.activation(out=squares[:], in_=b[j], func=ACT.Square, accum_out=sums[j])
                nc.gpsimd.tensor_scalar(
                    denominators[pair][:, i : i + 1], sums[j], -1.0, minus_tenth[:], ALU.mult, ALU.add
                )
                r[j] = r_of_pair[pair][:, i : i + 1]

        factor = [keep.tile([P, 1], F32, name=f"factor{j}") for j in range(BLOCKS)]
        y = [keep.tile([P, N], F32, name=f"y{j}") for j in range(BLOCKS)]

        def invert(pair):
            nc.vector.reciprocal(r_of_pair[pair], denominators[pair][:])

        def project(j):
            nc.vector.scalar_tensor_tensor(y[j][:], a_banks[j][:], r[j], b[j], ALU.mult, ALU.mult, accum_out=factor[j][:])

        def finish(j, pieces):
            for i in range(pieces):
                cols = slice(i * N // pieces, (i + 1) * N // pieces)
                nc.vector.scalar_tensor_tensor(
                    y[j][:, cols], b[j][:, cols], factor[j][:], a_banks[j][:, cols], ALU.mult, ALU.add
                )
                nc.sync.dma_start(out=out[j * P : (j + 1) * P, cols], in_=y[j][:, cols])

        def finish_aside(j):
            a_copy = keep.tile([P, N], F32, name="a_copy")
            part = keep.tile([P, N], F32, name="part")
            nc.scalar.copy(out=a_copy[:], in_=a_banks[j][:])
            nc.gpsimd.tensor_scalar(part[:], b[j], factor[j][:], 0.0, ALU.mult, ALU.add)
            nc.gpsimd.tensor_tensor(y[j][:], part[:], a_copy[:], ALU.add)
            nc.sync.dma_start(out=out[j * P : (j + 1) * P, :], in_=y[j][:])

        invert(early_pair)
        project(0)
        finish_aside(0)
        project(1)
        invert(late_pair)
        finish(1, pieces=1)
        project(2)
        project(3)
        finish(2, pieces=1)
        finish(3, pieces=2)
